import numpy as np
import ml_dtypes


def mxq(x, axis, fmt="e4m3"):
    dtype, down = {"e4m3": (ml_dtypes.float8_e4m3fn, 7), "e5m2": (ml_dtypes.float8_e5m2, 14)}[fmt]
    v = np.moveaxis(np.asarray(x, np.float32).astype(ml_dtypes.bfloat16).astype(np.float64), axis, -1)
    blocks = v.reshape(v.shape[:-1] + (-1, 32))
    amax = np.abs(blocks).max(-1, keepdims=True)
    byte = np.maximum(np.where(amax > 0, np.frexp(amax)[1] - 1 + 127, 0) - down, 1)
    scale = np.exp2(byte - 127.0)
    codes = (blocks / scale).astype(np.float32).astype(dtype).astype(np.float64)
    return np.moveaxis((codes * scale).reshape(v.shape), -1, axis)


WIDE = False


def mx_kscale(k):
    if not WIDE:
        return np.ones(k)
    levels = np.array([10, -10, 5, -5, 0])
    if k % 512:
        return np.exp2(np.random.permutation(np.resize(levels, k // 32))).repeat(32)
    a = np.empty((k // 512, 16))
    for p in range(k // 512):
        a[p, :8] = np.random.permutation(np.resize(levels, 8))
        for g in range(8):
            far = levels[np.abs(levels - a[p, g]) >= 10]
            a[p, g + 8] = far[np.random.randint(len(far))]
    return np.exp2(a.ravel()).repeat(32)


def f64(x):
    return np.asarray(x).astype(np.float64)


def striped(idx):
    return np.tile(idx.reshape(-1, 16).T, (8, 1)).astype(np.uint16)


def unstriped(offs):
    return offs[:16].T.reshape(-1).astype(np.int64)


E2M1 = np.array([0.0, 0.5, 1.0, 1.5, 2.0, 3.0, 4.0, 6.0, -0.0, -0.5, -1.0, -1.5, -2.0, -3.0, -4.0, -6.0])


def pack_weight(w, fmt):
    k, n = w.shape
    w = f64(np.asarray(w, np.float32).astype(ml_dtypes.bfloat16)).reshape(k // 32, 32, n)
    amax = np.abs(w).max(1)
    if fmt == "e4m3":
        byte = np.frexp(amax)[1] - 1 + 127 - 7
    else:
        mant, ex = np.frexp(amax / 6.0)
        byte = np.where(mant > 0.5, ex, ex - 1) + 127
    byte = np.clip(np.where(amax > 0, byte, 1), 1, 254)
    scaled = (w * np.exp2(127.0 - byte)[:, None, :]).reshape(k, n).astype(np.float32)
    by_word = np.ascontiguousarray(scaled.reshape(k // 512, 128, 4, n).transpose(0, 1, 3, 2))
    if fmt == "e4m3":
        words = by_word.astype(ml_dtypes.float8_e4m3fn).view(np.uint8)
    else:
        c = by_word.astype(ml_dtypes.float4_e2m1fn).view(np.uint8) & 0xF
        words = (c[..., 0::2] | (c[..., 1::2] << 4)).reshape(k // 512, 128, 2 * n)
    return np.ascontiguousarray(words), np.ascontiguousarray(byte.astype(np.uint8).reshape(k // 512, 16, n))


def unpack_weight(words, scales, fmt):
    g, _, n = scales.shape
    words = np.ascontiguousarray(words).reshape(g, 128, n, -1)
    if fmt == "e4m3":
        vals = words.view(ml_dtypes.float8_e4m3fn).astype(np.float64)
    else:
        nib = np.empty((g, 128, n, 4), np.uint8)
        nib[..., 0::2] = words & 0xF
        nib[..., 1::2] = words >> 4
        vals = E2M1[nib]
    vals = vals * np.repeat(np.exp2(scales.astype(np.float64) - 127.0), 8, axis=1)[..., None]
    return vals.transpose(0, 1, 3, 2).reshape(g * 512, n)


def gelu(v):
    return 0.5 * v * (1.0 + np.tanh(np.sqrt(2.0 / np.pi) * (v + 0.044715 * v**3)))


K, T, S, T2, H, N, R = 512, 2048, 1024, 2048, 1024, 384, 128

def setup_inputs():
    n = np.random.standard_normal
    s = mx_kscale(K)[:, None]
    u = mx_kscale(H)[:, None]
    tab_words, tab_scales = pack_weight(n((K, T)) * s, "e4m3")
    wr_words, wr_scales = pack_weight(n((K, H)) / np.sqrt(K) / s * u.T, "e2m1")
    return {
        "tab_words": tab_words, "tab_scales": tab_scales,
        "offs": striped(np.random.permutation(T)[:S]),
        "wl": (n((K, H)) / np.sqrt(K) / s * u.T).astype(np.float32),
        "wr_words": wr_words, "wr_scales": wr_scales,
        "offs2": striped(np.random.permutation(T2)[:S]),
        "offs3": striped(np.random.permutation(T2)[:S]),
        "wg1": np.exp(0.3 * n((R, S))).astype(np.float32),
        "wg2": np.exp(0.3 * n((R, S))).astype(np.float32),
        "rest": (0.8 * n((H, T2)) * u).astype(np.float32),
        "wd": (n((H, N)) / np.sqrt(H) / (u * u)).astype(np.float32),
    }

def reference(tab_words, tab_scales, offs, wl, wr_words, wr_scales, offs2, offs3, wg1, wg2, rest, wd):
    v = unpack_weight(tab_words, tab_scales, "e4m3")[:, unstriped(offs)]
    wr = unpack_weight(wr_words, wr_scales, "e2m1")
    h1 = mxq(f64(wl), 0, "e4m3").T @ v
    h2 = wr.T @ v
    pageA = np.zeros((H, T2))
    pageA[:, unstriped(offs2)] = np.tile(f64(wg1), (H // R, 1)) * h1
    pageB = np.zeros((H, T2))
    pageB[:, unstriped(offs3)] = np.tile(f64(wg2), (H // R, 1)) * h2
    z = np.square(pageA + pageB + f64(rest))
    return mxq(f64(wd), 0, "e4m3").T @ mxq(z, 0, "e4m3")

@@ -1,0 +1,255 @@
+from contextlib import ExitStack
+
+import concourse.mybir as mybir
+from concourse.masks import make_identity
+
+K, T, S, T2, H, N = 512, 2048, 1024, 2048, 1024, 384
+FLOPS = 2 * 2 * K * H * S + 2 * H * N * T2
+
+F32 = mybir.dt.float32
+BF16 = mybir.dt.bfloat16
+I32 = mybir.dt.int32
+U32 = mybir.dt.uint32
+U16 = mybir.dt.uint16
+U8 = mybir.dt.uint8
+FP8X4 = mybir.dt.float8_e4m3fn_x4
+FP4X4 = mybir.dt.float4_e2m1fn_x4
+MULT = mybir.AluOpType.mult
+SQUARE = mybir.ActivationFunctionType.Square
+
+P = 128
+BANK = 512
+SLICES = H // P
+PASS_SLICES = 4
+CHUNKS = T2 // BANK
+TILES = BANK // P
+N_TILES = N // P
+WL_PIECES = ((0, 128), (128, 256), (256, 512), (512, 1024))
+
+
+def tile_list_binocular_fusion_readout_kernel(
+    tc, tab_words, tab_scales, offs, wl, wr_words, wr_scales, offs2, offs3, wg1, wg2, rest, wd, out
+):
+    nc = tc.nc
+    with ExitStack() as ctx:
+        lists = ctx.enter_context(tc.tile_pool(name="lists", bufs=1))
+        keep = ctx.enter_context(tc.tile_pool(name="keep", bufs=1))
+        ring = ctx.enter_context(tc.tile_pool(name="ring", bufs=2))
+        psum = ctx.enter_context(tc.psum_pool(name="psum", bufs=1))
+
+        def kept(name, shape, dtype):
+            return keep.tile(shape, dtype, name=name, tag=name, align_bytes=64)
+
+        banks = [psum.tile([P, BANK], F32, name="bank%d" % b) for b in range(8)]
+        sum_banks, h_banks, turn_banks = banks[0:4], banks[4:6], banks[6:8]
+
+        idx = lists.tile([P, S // 16], U16, name="idx")
+        idx_a = lists.tile([P, S // 16], U16, name="idx_a")
+        idx_b = lists.tile([P, S // 16], U16, name="idx_b")
+
+        def load_scale_rows(queue, plane, rows):
+            for q in range(4):
+                queue.dma_start(
+                    out=plane[32 * q : 32 * q + 4, :].bitcast(I32), in_=rows[0, 4 * q : 4 * q + 4, :].bitcast(I32)
+                )
+
+        tab_s = kept("tab_s", [P, T], U8)
+        tab_w = kept("tab_w", [P, T], I32)
+        page_a = kept("page_a", [P, T2], F32)
+        page_b = kept("page_b", [P, T2], F32)
+        wr_s = kept("wr_s", [P, H], U8)
+        wr_w = kept("wr_w", [P, 2 * H], U8)
+        ident = kept("ident", [P, P], F32)
+        nc.gpsimd.memset(tab_s[:].bitcast(I32), 0)
+        nc.vector.memset(page_a[:], 0.0)
+        make_identity(nc, ident[:])
+        nc.gpsimd.memset(wr_s[:].bitcast(I32), 0)
+        nc.gpsimd.memset(page_b[:], 0.0)
+
+        nc.sync.dma_start(idx[:], offs)
+        nc.sync.dma_start(idx_a[:], offs2)
+        nc.sync.dma_start(idx_b[:], offs3)
+        load_scale_rows(nc.scalar, tab_s, tab_scales)
+        nc.sync.dma_start(out=tab_w[:], in_=tab_words[0].rearrange("p t i -> p (t i)").bitcast(I32))
+
+        wl_c = kept("wl_c", [P, H], U32)
+        wl_s = kept("wl_s", [P, H], U8)
+
+        def load_k_first(name, rows):
+            raw = kept(name, [P, 4, rows.shape[1]], F32)
+            nc.sync.dma_start(out=raw[:], in_=rows.rearrange("(p j) c -> p j c", j=4))
+            return raw
+
+        def quantize(codes, scales, grouped):
+            nc.vector.quantize_mx(out=codes.bitcast(FP8X4), scales=scales, in_=grouped)
+
+        def quantize_wl(piece):
+            c0, c1 = WL_PIECES[piece]
+            raw = load_k_first("wl_raw%d" % piece, wl[:, c0:c1])
+            grouped = kept("wl_g%d" % piece, [P, c1 - c0, 4], BF16)
+            nc.scalar.copy(out=grouped[:], in_=raw[:].rearrange("p j c -> p c j"))
+            quantize(wl_c[:, c0:c1], wl_s[:, c0:c1], grouped[:].rearrange("p c j -> p (c j)"))
+
+        quantize_wl(0)
+        gain_a = kept("gain_a", [P, S], F32)
+        nc.sync.dma_start(out=gain_a[:], in_=wg1)
+
+        v_w = kept("v_w", [P, S], U32)
+        v_s = kept("v_s", [P, S], U8)
+        halves = [(slice(BANK * u, BANK * (u + 1)), slice(32 * u, 32 * (u + 1))) for u in range(2)]
+        for entries, columns in halves:
+            nc.vector.tensor_copy(v_s[:, entries], tab_s[:].indirect(idx[:, columns]))
+        for entries, columns in halves:
+            nc.vector.tensor_copy(v_w[:, entries], tab_w[:].bitcast(U32).indirect(idx[:, columns]))
+
+        nc.sync.dma_start(out=wr_w[:].bitcast(I32), in_=wr_words[0].bitcast(I32))
+        load_scale_rows(nc.sync, wr_s, wr_scales)
+        gain_b = kept("gain_b", [P, S], F32)
+        nc.sync.dma_start(out=gain_b[:], in_=wg2)
+
+        def load_rest(s):
+            rows = ring.tile([P, T2], F32, name="rest_rows", tag="rest_rows", bufs=3)
+            nc.sync.dma_start(out=rows[:], in_=rest[P * s : P * (s + 1), :])
+            return rows
+
+        rest_rows = {0: load_rest(0)}
+        for piece in range(1, len(WL_PIECES)):
+            quantize_wl(piece)
+        rest_rows[1] = load_rest(1)
+        wd_g = kept("wd_g", [P, 2 * N, 4], BF16)
+        for b in range(2):
+            raw = load_k_first("wd_raw%d" % b, wd[K * b : K * (b + 1), :])
+            nc.scalar.copy(out=wd_g[:, N * b : N * (b + 1), :], in_=raw[:].rearrange("p j c -> p c j"))
+        rest_rows[2] = load_rest(2)
+
+        def drive(name, codes, scales):
+            h = ring.tile([P, S], F32, name=name, tag=name)
+            for bank, (entries, columns) in zip(h_banks, halves):
+                nc.tensor.matmul_mx(
+                    out=bank[:], lhsT=codes, lhsT_scale=scales,
+                    rhs=v_w[:, entries].bitcast(FP8X4), rhs_scale=v_s[:, entries], start=True, stop=True,
+                )
+                nc.scalar.copy(out=h[:, entries], in_=bank[:])
+            return h
+
+        def drive_a(s):
+            return drive("h_a", wl_c[:, P * s : P * (s + 1)].bitcast(FP8X4), wl_s[:, P * s : P * (s + 1)])
+
+        def drive_b(s):
+            return drive("h_b", wr_w[:, 2 * P * s : 2 * P * (s + 1)].bitcast(FP4X4), wr_s[:, P * s : P * (s + 1)])
+
+        def add_turned(source, c, first=False, last=False):
+            for j in range(TILES):
+                m0 = BANK * c + P * j
+                nc.tensor.matmul(
+                    sum_banks[c][:, P * j : P * (j + 1)], source[:, m0 : m0 + P], ident[:],
+                    start=(first and j == 0), stop=(last and j == TILES - 1), is_transpose=True,
+                )
+
+        z_turned = {}
+
+        def square(s, c):
+            b, q = divmod(s, PASS_SLICES)
+            if q == 0:
+                z_turned[b, c] = kept("z_turned%d_%d" % (b, c), [P, TILES, 2, P, 2], BF16)
+            nc.scalar.activation(
+                out=z_turned[b, c][:, :, :, 32 * q : 32 * (q + 1), :].rearrange("m j u p e -> m u j p e"),
+                in_=sum_banks[c][:].rearrange("m (j p u e) -> m u j p e", j=TILES, u=2, e=2),
+                func=SQUARE,
+            )
+
+        def turn_back(b, c, pair, grouped, copies):
+            words = z_turned[b, c][:].rearrange("m j u p e -> m (j u p e)").bitcast(F32)
+            target = grouped[:].bitcast(F32).rearrange("p (h j m u) -> p h j m u", h=2, j=2, u=2)
+            for half in range(2):
+                for i in range(4):
+                    w0 = BANK * half + P * i
+                    nc.tensor.transpose(pair[half][:, P * i : P * (i + 1)], words[:, w0 : w0 + P], ident[:])
+                copies[half](
+                    out=target[:, half], in_=pair[half][:].rearrange("p (j u m) -> p j m u", j=2, u=2)
+                )
+
+        def scatter(page, offsets, h, gain):
+            nc.vector.tensor_tensor(page[:].indirect(offsets), h, gain, MULT)
+
+        z_g = {}
+        h_a, h_b = drive_a(0), drive_b(0)
+        for s in range(SLICES):
+            if s == 0:
+                for entries, columns in halves:
+                    scatter(page_a, idx_a[:, columns], h_a[:, entries], gain_a[:, entries])
+            else:
+                scatter(page_a, idx_a[:], h_a[:], gain_a[:])
+                for c in range(CHUNKS):
+                    add_turned(page_b, c, last=True)
+                    square(s - 1, c)
+            if s + 1 < SLICES:
+                h_a = drive_a(s + 1)
+            for c in range(CHUNKS):
+                add_turned(rest_rows[s], c, first=True)
+            if s + 3 < SLICES:
+                rest_rows[s + 3] = load_rest(s + 3)
+            scatter(page_b, idx_b[:], h_b[:], gain_b[:])
+            for c in range(CHUNKS):
+                add_turned(page_a, c)
+            if s + 1 < SLICES:
+                h_b = drive_b(s + 1)
+            if s >= PASS_SLICES:
+                c = s - PASS_SLICES
+                z_g[0, c] = kept("z_g0_%d" % c, [P, 4 * BANK], BF16)
+                turn_back(0, c, turn_banks, z_g[0, c], (nc.scalar.copy, nc.scalar.copy))
+
+        late_c = kept("gain_b", [P, 2 * N + T2], U32)
+        wd_c, z0_c = late_c[:, : 2 * N], late_c[:, 2 * N :]
+        z1_c = kept("z1_c", [P, T2], U32)
+        wd_s = kept("wd_s", [P, 2 * N], U8)
+        z_s = kept("z_s", [P, 2, T2], U8)
+        wd_flat = wd_g[:].rearrange("p c j -> p (c j)")
+        z_c = (z0_c, z1_c[:])
+        out_banks = ((banks[4], banks[5], banks[0]), (banks[3], banks[6], banks[7]))
+
+        def quantize_z(b, c):
+            columns = slice(BANK * c, BANK * (c + 1))
+            quantize(z_c[b][:, columns], z_s[:, b, columns], z_g[b, c][:])
+
+        def read_out(b, c):
+            columns = slice(BANK * c, BANK * (c + 1))
+            for t, bank in enumerate(out_banks[c % 2]):
+                n = slice(N * b + P * t, N * b + P * (t + 1))
+                nc.tensor.matmul_mx(
+                    out=bank[:], lhsT=wd_c[:, n].bitcast(FP8X4), lhsT_scale=wd_s[:, n],
+                    rhs=z_c[b][:, columns].bitcast(FP8X4), rhs_scale=z_s[:, b, columns],
+                    start=(b == 0), stop=(b == 1),
+                )
+
+        def store(c):
+            for t, bank in enumerate(out_banks[c % 2]):
+                staged = ring.tile([P, BANK], F32, name="staged", tag="staged", bufs=6)
+                copy = nc.vector.tensor_copy if (t == 1 and c > 0) else nc.scalar.copy
+                copy(out=staged[:], in_=bank[:])
+                nc.sync.dma_start(out=out[P * t : P * (t + 1), BANK * c : BANK * (c + 1)], in_=staged[:])
+
+        def turn_last(c):
+            z_g[1, c] = ring.tile([P, 4 * BANK], BF16, name="z_g1", tag="z_g1", align_bytes=64)
+            pair = turn_banks if c == 0 else banks[1:3]
+            turn_back(1, c, pair, z_g[1, c], (nc.scalar.copy, nc.vector.tensor_copy))
+            quantize_z(1, c)
+
+        quantize(wd_c[:, :BANK], wd_s[:, :BANK], wd_flat[:, : 4 * BANK])
+        quantize_z(0, 0)
+        quantize(wd_c[:, BANK:], wd_s[:, BANK:], wd_flat[:, 4 * BANK :])
+        quantize_z(0, 1)
+        for c in range(CHUNKS):
+            add_turned(page_b, c, last=True)
+            square(SLICES - 1, c)
+        read_out(0, 0)
+        turn_last(0)
+        for c in range(CHUNKS):
+            if c + 1 < CHUNKS:
+                turn_last(c + 1)
+            if c + 2 < CHUNKS:
+                quantize_z(0, c + 2)
+            read_out(1, c)
+            if c + 1 < CHUNKS:
+                read_out(0, c + 1)
+            store(c)

@@ -1,7 +1,6 @@
 from contextlib import ExitStack
 
 import concourse.mybir as mybir
-from concourse.masks import make_identity
 
 K, T, S, T2, H, N = 512, 2048, 1024, 2048, 1024, 384
 FLOPS = 2 * 2 * K * H * S + 2 * H * N * T2
@@ -24,7 +23,8 @@ PASS_SLICES = 4
 CHUNKS = T2 // BANK
 TILES = BANK // P
 N_TILES = N // P
-WL_PIECES = ((0, 128), (128, 256), (256, 512), (512, 1024))
+WL_PIECES = ((0, 256), (256, 512), (512, 1024))
+WL_FIRST = WL_PIECES[0][1]
 
 
 def tile_list_binocular_fusion_readout_kernel(
@@ -54,45 +54,45 @@ def tile_list_binocular_fusion_readout_kernel(
                 )
 
         tab_s = kept("tab_s", [P, T], U8)
-        tab_w = kept("tab_w", [P, T], I32)
-        page_a = kept("page_a", [P, T2], F32)
-        page_b = kept("page_b", [P, T2], F32)
-        wr_s = kept("wr_s", [P, H], U8)
-        wr_w = kept("wr_w", [P, 2 * H], U8)
         ident = kept("ident", [P, P], F32)
         nc.gpsimd.memset(tab_s[:].bitcast(I32), 0)
-        nc.vector.memset(page_a[:], 0.0)
-        make_identity(nc, ident[:])
-        nc.gpsimd.memset(wr_s[:].bitcast(I32), 0)
-        nc.gpsimd.memset(page_b[:], 0.0)
-
-        nc.sync.dma_start(idx[:], offs)
-        nc.sync.dma_start(idx_a[:], offs2)
-        nc.sync.dma_start(idx_b[:], offs3)
-        load_scale_rows(nc.scalar, tab_s, tab_scales)
-        nc.sync.dma_start(out=tab_w[:], in_=tab_words[0].rearrange("p t i -> p (t i)").bitcast(I32))
+        zeros = kept("tab_w", [P, P], F32)
+        nc.gpsimd.memset(zeros[:], 0.0)
+        nc.gpsimd.affine_select(
+            out=ident[:], in_=zeros[:], pattern=[[-1, P]],
+            compare_op=mybir.AluOpType.not_equal, fill=1.0, base=0, channel_multiplier=1,
+        )
+        page_a = kept("page_a", [P, T2], F32)
+        nc.vector.memset(page_a[:].bitcast(I32), 0)
 
         wl_c = kept("wl_c", [P, H], U32)
         wl_s = kept("wl_s", [P, H], U8)
 
-        def load_k_first(name, rows):
-            raw = kept(name, [P, 4, rows.shape[1]], F32)
-            nc.sync.dma_start(out=raw[:], in_=rows.rearrange("(p j) c -> p j c", j=4))
-            return raw
+        def load_k_first(raw, rows):
+            nc.sync.dma_start(out=raw, in_=rows.rearrange("(p j) c -> p j c", j=4))
 
         def quantize(codes, scales, grouped):
             nc.vector.quantize_mx(out=codes.bitcast(FP8X4), scales=scales, in_=grouped)
 
-        def quantize_wl(piece):
+        def quantize_wl(piece, raw):
             c0, c1 = WL_PIECES[piece]
-            raw = load_k_first("wl_raw%d" % piece, wl[:, c0:c1])
             grouped = kept("wl_g%d" % piece, [P, c1 - c0, 4], BF16)
-            nc.scalar.copy(out=grouped[:], in_=raw[:].rearrange("p j c -> p c j"))
+            nc.scalar.copy(out=grouped[:], in_=raw.rearrange("p j c -> p c j"))
             quantize(wl_c[:, c0:c1], wl_s[:, c0:c1], grouped[:].rearrange("p c j -> p (c j)"))
 
-        quantize_wl(0)
-        gain_a = kept("gain_a", [P, S], F32)
-        nc.sync.dma_start(out=gain_a[:], in_=wg1)
+        nc.sync.dma_start(idx[:], offs)
+        nc.sync.dma_start(idx_a[:], offs2)
+        nc.sync.dma_start(idx_b[:], offs3)
+        load_scale_rows(nc.sync, tab_s, tab_scales)
+        wl_first = kept("wl_first", [P, 4, WL_FIRST], F32)
+        load_k_first(wl_first[:], wl[:, :WL_FIRST])
+        tab_w = kept("tab_w", [P, T], I32)
+        nc.sync.dma_start(out=tab_w[:], in_=tab_words[0].rearrange("p t i -> p (t i)").bitcast(I32))
+        quantize_wl(0, wl_first[:])
+        gains = kept("wl_g0", [P, 2 * S + 2 * T2], F32)
+        gain_a, gain_b, stream = gains[:, :S], gains[:, S : 2 * S], gains[:, 2 * S :]
+        nc.sync.dma_start(out=gain_a, in_=wg1)
+        nc.sync.dma_start(out=gain_b, in_=wg2)
 
         v_w = kept("v_w", [P, S], U32)
         v_s = kept("v_s", [P, S], U8)
@@ -102,41 +102,56 @@ def tile_list_binocular_fusion_readout_kernel(
         for entries, columns in halves:
             nc.vector.tensor_copy(v_w[:, entries], tab_w[:].bitcast(U32).indirect(idx[:, columns]))
 
+        wr_s = kept("tab_s", [P, H], U8)
+        nc.gpsimd.memset(wr_s[:].bitcast(I32), 0)
+        load_scale_rows(nc.gpsimd, wr_s, wr_scales)
+        page_b = kept("tab_w", [P, T2], F32)
+        nc.gpsimd.memset(page_b[:], 0.0)
+        wr_w = kept("wr_w", [P, 2 * H], U8)
         nc.sync.dma_start(out=wr_w[:].bitcast(I32), in_=wr_words[0].bitcast(I32))
-        load_scale_rows(nc.sync, wr_s, wr_scales)
-        gain_b = kept("gain_b", [P, S], F32)
-        nc.sync.dma_start(out=gain_b[:], in_=wg2)
+        wd_g = kept("wd_g", [P, 2, 4 * N], BF16)
+        rest_rows = {}
 
-        def load_rest(s):
-            rows = ring.tile([P, T2], F32, name="rest_rows", tag="rest_rows", bufs=3)
-            nc.sync.dma_start(out=rows[:], in_=rest[P * s : P * (s + 1), :])
-            return rows
+        def load_rest(s, slot):
+            rest_rows[s] = stream[:, T2 * slot : T2 * (slot + 1)]
+            nc.sync.dma_start(out=rest_rows[s], in_=rest[P * s : P * (s + 1), :])
 
-        rest_rows = {0: load_rest(0)}
-        for piece in range(1, len(WL_PIECES)):
-            quantize_wl(piece)
-        rest_rows[1] = load_rest(1)
-        wd_g = kept("wd_g", [P, 2 * N, 4], BF16)
-        for b in range(2):
-            raw = load_k_first("wd_raw%d" % b, wd[K * b : K * (b + 1), :])
-            nc.scalar.copy(out=wd_g[:, N * b : N * (b + 1), :], in_=raw[:].rearrange("p j c -> p c j"))
-        rest_rows[2] = load_rest(2)
+        def load_wl(piece, slot):
+            c0, c1 = WL_PIECES[piece]
+            raw = stream[:, T2 * slot : T2 * slot + 4 * (c1 - c0)].rearrange("p (j c) -> p j c", j=4)
+            load_k_first(raw, wl[:, c0:c1])
+            quantize_wl(piece, raw)
 
-        def drive(name, codes, scales):
-            h = ring.tile([P, S], F32, name=name, tag=name)
-            for bank, (entries, columns) in zip(h_banks, halves):
+        def load_wd(b, slot):
+            raw = stream[:, T2 * slot : T2 * slot + 4 * N].rearrange("p (j c) -> p j c", j=4)
+            load_k_first(raw, wd[K * b : K * (b + 1), :])
+            nc.scalar.copy(out=wd_g[:, b, :].rearrange("p (c j) -> p c j", j=4), in_=raw.rearrange("p j c -> p c j"))
+
+        load_rest(0, 0)
+        load_wl(1, 1)
+        load_rest(1, 1)
+
+        def drive(targets, codes, scales):
+            for bank, target, (entries, columns) in zip(h_banks, targets, halves):
                 nc.tensor.matmul_mx(
                     out=bank[:], lhsT=codes, lhsT_scale=scales,
                     rhs=v_w[:, entries].bitcast(FP8X4), rhs_scale=v_s[:, entries], start=True, stop=True,
                 )
-                nc.scalar.copy(out=h[:, entries], in_=bank[:])
-            return h
+                nc.scalar.copy(out=target, in_=bank[:])
 
         def drive_a(s):
-            return drive("h_a", wl_c[:, P * s : P * (s + 1)].bitcast(FP8X4), wl_s[:, P * s : P * (s + 1)])
+            h = ring.tile([P, S], F32, name="h_a", tag="h_a")
+            drive([h[:, :BANK], h[:, BANK:]], wl_c[:, P * s : P * (s + 1)].bitcast(FP8X4), wl_s[:, P * s : P * (s + 1)])
+            return h
 
         def drive_b(s):
-            return drive("h_b", wr_w[:, 2 * P * s : 2 * P * (s + 1)].bitcast(FP4X4), wr_s[:, P * s : P * (s + 1)])
+            if s + 1 < SLICES:
+                h = ring.tile([P, S], F32, name="h_b", tag="h_b")
+                targets = [h[:, :BANK], h[:, BANK:]]
+            else:
+                h = targets = [kept("h_last%d" % u, [P, BANK], F32)[:] for u in range(2)]
+            drive(targets, wr_w[:, 2 * P * s : 2 * P * (s + 1)].bitcast(FP4X4), wr_s[:, P * s : P * (s + 1)])
+            return h
 
         def add_turned(source, c, first=False, last=False):
             for j in range(TILES):
@@ -173,13 +188,34 @@ def tile_list_binocular_fusion_readout_kernel(
             nc.vector.tensor_tensor(page[:].indirect(offsets), h, gain, MULT)
 
         z_g = {}
+        wd_s = kept("wd_s", [P, 2, N], U8)
+        z_s = kept("z_s", [P, 2, T2], U8)
+        wd_c, z_c = {}, {}
+        out_banks = ((banks[4], banks[5], banks[6]), (banks[3], banks[7], banks[0]))
+
+        def quantize_wd(b):
+            for n0, n1 in ((0, 2 * P), (2 * P, N)):
+                quantize(wd_c[b][:, n0:n1], wd_s[:, b, n0:n1], wd_g[:, b, 4 * n0 : 4 * n1])
+
+        def quantize_z(b, c):
+            quantize(z_c[b, c], z_s[:, b, BANK * c : BANK * (c + 1)], z_g[b, c][:])
+
+        def read_out(b, c):
+            for t, bank in enumerate(out_banks[c % 2]):
+                n = slice(P * t, P * (t + 1))
+                nc.tensor.matmul_mx(
+                    out=bank[:], lhsT=wd_c[b][:, n].bitcast(FP8X4), lhsT_scale=wd_s[:, b, n],
+                    rhs=z_c[b, c].bitcast(FP8X4), rhs_scale=z_s[:, b, BANK * c : BANK * (c + 1)],
+                    start=(b == 0), stop=(b == 1),
+                )
+
         h_a, h_b = drive_a(0), drive_b(0)
         for s in range(SLICES):
             if s == 0:
                 for entries, columns in halves:
                     scatter(page_a, idx_a[:, columns], h_a[:, entries], gain_a[:, entries])
             else:
-                scatter(page_a, idx_a[:], h_a[:], gain_a[:])
+                scatter(page_a, idx_a[:], h_a[:], gain_a)
                 for c in range(CHUNKS):
                     add_turned(page_b, c, last=True)
                     square(s - 1, c)
@@ -187,69 +223,73 @@ def tile_list_binocular_fusion_readout_kernel(
                 h_a = drive_a(s + 1)
             for c in range(CHUNKS):
                 add_turned(rest_rows[s], c, first=True)
-            if s + 3 < SLICES:
-                rest_rows[s + 3] = load_rest(s + 3)
-            scatter(page_b, idx_b[:], h_b[:], gain_b[:])
+            if s == 1:
+                load_wl(2, 1)
+            if s + 2 < SLICES:
+                load_rest(s + 2, s % 2)
+            if s == SLICES - 2:
+                load_wd(0, 0)
+                load_wd(1, 0)
+            if s + 1 < SLICES:
+                scatter(page_b, idx_b[:], h_b[:], gain_b)
             for c in range(CHUNKS):
                 add_turned(page_a, c)
             if s + 1 < SLICES:
                 h_b = drive_b(s + 1)
-            if s >= PASS_SLICES:
-                c = s - PASS_SLICES
-                z_g[0, c] = kept("z_g0_%d" % c, [P, 4 * BANK], BF16)
-                turn_back(0, c, turn_banks, z_g[0, c], (nc.scalar.copy, nc.scalar.copy))
+            if s in (PASS_SLICES, PASS_SLICES + 1):
+                for c in (2 * (s - PASS_SLICES), 2 * (s - PASS_SLICES) + 1):
+                    z_g[0, c] = kept("z_g0_%d" % c, [P, 4 * BANK], BF16)
+                    turn_back(0, c, turn_banks, z_g[0, c], (nc.scalar.copy, nc.scalar.copy))
 
-        late_c = kept("gain_b", [P, 2 * N + T2], U32)
-        wd_c, z0_c = late_c[:, : 2 * N], late_c[:, 2 * N :]
+        (entries, columns), (last_entries, last_columns) = halves
+        scatter(page_b, idx_b[:, columns], h_b[0], gain_b[:, entries])
+        early_c = kept("h_last0", [P, N + BANK], U32)
+        wd_c[0], z_c[0, 0] = early_c[:, :N], early_c[:, N:]
+        quantize_wd(0)
+        quantize_z(0, 0)
+        read_out(0, 0)
+        scatter(page_b, idx_b[:, last_columns], h_b[1], gain_b[:, last_entries])
+
+        late_c = kept("wl_g0", [P, N + T2 - BANK], U32)
+        wd_c[1] = late_c[:, :N]
         z1_c = kept("z1_c", [P, T2], U32)
-        wd_s = kept("wd_s", [P, 2 * N], U8)
-        z_s = kept("z_s", [P, 2, T2], U8)
-        wd_flat = wd_g[:].rearrange("p c j -> p (c j)")
-        z_c = (z0_c, z1_c[:])
-        out_banks = ((banks[4], banks[5], banks[0]), (banks[3], banks[6], banks[7]))
-
-        def quantize_z(b, c):
-            columns = slice(BANK * c, BANK * (c + 1))
-            quantize(z_c[b][:, columns], z_s[:, b, columns], z_g[b, c][:])
-
-        def read_out(b, c):
-            columns = slice(BANK * c, BANK * (c + 1))
-            for t, bank in enumerate(out_banks[c % 2]):
-                n = slice(N * b + P * t, N * b + P * (t + 1))
-                nc.tensor.matmul_mx(
-                    out=bank[:], lhsT=wd_c[:, n].bitcast(FP8X4), lhsT_scale=wd_s[:, n],
-                    rhs=z_c[b][:, columns].bitcast(FP8X4), rhs_scale=z_s[:, b, columns],
-                    start=(b == 0), stop=(b == 1),
-                )
+        for c in range(CHUNKS):
+            z_c[1, c] = z1_c[:, BANK * c : BANK * (c + 1)]
+            if c > 0:
+                z_c[0, c] = late_c[:, N + BANK * (c - 1) : N + BANK * c]
 
         def store(c):
             for t, bank in enumerate(out_banks[c % 2]):
                 staged = ring.tile([P, BANK], F32, name="staged", tag="staged", bufs=6)
-                copy = nc.vector.tensor_copy if (t == 1 and c > 0) else nc.scalar.copy
+                copy = nc.vector.tensor_copy if t == 1 else nc.scalar.copy
                 copy(out=staged[:], in_=bank[:])
                 nc.sync.dma_start(out=out[P * t : P * (t + 1), BANK * c : BANK * (c + 1)], in_=staged[:])
 
         def turn_last(c):
             z_g[1, c] = ring.tile([P, 4 * BANK], BF16, name="z_g1", tag="z_g1", align_bytes=64)
-            pair = turn_banks if c == 0 else banks[1:3]
+            pair = (banks[7], banks[0]) if c == 0 else banks[1:3]
             turn_back(1, c, pair, z_g[1, c], (nc.scalar.copy, nc.vector.tensor_copy))
             quantize_z(1, c)
 
-        quantize(wd_c[:, :BANK], wd_s[:, :BANK], wd_flat[:, : 4 * BANK])
-        quantize_z(0, 0)
-        quantize(wd_c[:, BANK:], wd_s[:, BANK:], wd_flat[:, 4 * BANK :])
         quantize_z(0, 1)
+        quantize_wd(1)
+        quantize_z(0, 2)
         for c in range(CHUNKS):
             add_turned(page_b, c, last=True)
             square(SLICES - 1, c)
-        read_out(0, 0)
         turn_last(0)
-        for c in range(CHUNKS):
-            if c + 1 < CHUNKS:
-                turn_last(c + 1)
-            if c + 2 < CHUNKS:
-                quantize_z(0, c + 2)
-            read_out(1, c)
-            if c + 1 < CHUNKS:
-                read_out(0, c + 1)
-            store(c)
+        turn_last(1)
+        read_out(0, 1)
+        read_out(1, 0)
+        store(0)
+        turn_last(2)
+        quantize_z(0, 3)
+        read_out(1, 1)
+        store(1)
+        read_out(0, 2)
+        turn_last(3)
+        read_out(1, 2)
+        store(2)
+        read_out(0, 3)
+        read_out(1, 3)
+        store(3)

@@ -13,18 +13,18 @@ U16 = mybir.dt.uint16
 U8 = mybir.dt.uint8
 FP8X4 = mybir.dt.float8_e4m3fn_x4
 FP4X4 = mybir.dt.float4_e2m1fn_x4
-MULT = mybir.AluOpType.mult
-SQUARE = mybir.ActivationFunctionType.Square
 
 P = 128
+PACK = 4
 BANK = 512
+PER_COLUMN = 16
 SLICES = H // P
 PASS_SLICES = 4
 CHUNKS = T2 // BANK
 TILES = BANK // P
-N_TILES = N // P
 WL_PIECES = ((0, 256), (256, 512), (512, 1024))
 WL_FIRST = WL_PIECES[0][1]
+HEAD = 256
 
 
 def tile_list_binocular_fusion_readout_kernel(
@@ -37,15 +37,18 @@ def tile_list_binocular_fusion_readout_kernel(
         ring = ctx.enter_context(tc.tile_pool(name="ring", bufs=2))
         psum = ctx.enter_context(tc.psum_pool(name="psum", bufs=1))
 
-        def kept(name, shape, dtype):
-            return keep.tile(shape, dtype, name=name, tag=name, align_bytes=64)
+        def kept(slot, shape, dtype):
+            return keep.tile(shape, dtype, name=slot, tag=slot, align_bytes=64)
 
         banks = [psum.tile([P, BANK], F32, name="bank%d" % b) for b in range(8)]
         sum_banks, h_banks, turn_banks = banks[0:4], banks[4:6], banks[6:8]
 
-        idx = lists.tile([P, S // 16], U16, name="idx")
-        idx_a = lists.tile([P, S // 16], U16, name="idx_a")
-        idx_b = lists.tile([P, S // 16], U16, name="idx_b")
+        idx = lists.tile([P, S // PER_COLUMN], U16, name="idx")
+        idx_a = lists.tile([P, S // PER_COLUMN], U16, name="idx_a")
+        idx_b = lists.tile([P, S // PER_COLUMN], U16, name="idx_b")
+
+        def entries(offsets, e0, e1):
+            return offsets[:, e0 // PER_COLUMN : e1 // PER_COLUMN]
 
         def load_scale_rows(queue, plane, rows):
             for q in range(4):
@@ -53,30 +56,30 @@ def tile_list_binocular_fusion_readout_kernel(
                     out=plane[32 * q : 32 * q + 4, :].bitcast(I32), in_=rows[0, 4 * q : 4 * q + 4, :].bitcast(I32)
                 )
 
-        tab_s = kept("tab_s", [P, T], U8)
+        def load_k_first(raw, rows):
+            nc.sync.dma_start(out=raw, in_=rows.rearrange("(p j) c -> p j c", j=PACK))
+
+        def quantize(codes, scales, grouped):
+            nc.vector.quantize_mx(out=codes.bitcast(FP8X4), scales=scales, in_=grouped)
+
+        tab_s = kept("table_scales", [P, T], U8)
         ident = kept("ident", [P, P], F32)
-        nc.gpsimd.memset(tab_s[:].bitcast(I32), 0)
-        zeros = kept("tab_w", [P, P], F32)
+        zeros = kept("table_words", [P, P], F32)
         nc.gpsimd.memset(zeros[:], 0.0)
+        nc.gpsimd.memset(tab_s[:].bitcast(I32), 0)
         nc.gpsimd.affine_select(
             out=ident[:], in_=zeros[:], pattern=[[-1, P]],
             compare_op=mybir.AluOpType.not_equal, fill=1.0, base=0, channel_multiplier=1,
         )
         page_a = kept("page_a", [P, T2], F32)
-        nc.vector.memset(page_a[:].bitcast(I32), 0)
+        nc.gpsimd.memset(page_a[:], 0.0)
 
-        wl_c = kept("wl_c", [P, H], U32)
-        wl_s = kept("wl_s", [P, H], U8)
-
-        def load_k_first(raw, rows):
-            nc.sync.dma_start(out=raw, in_=rows.rearrange("(p j) c -> p j c", j=4))
-
-        def quantize(codes, scales, grouped):
-            nc.vector.quantize_mx(out=codes.bitcast(FP8X4), scales=scales, in_=grouped)
+        wl_c = kept("wl_codes", [P, H], U32)
+        wl_s = kept("wl_scales", [P, H], U8)
 
         def quantize_wl(piece, raw):
             c0, c1 = WL_PIECES[piece]
-            grouped = kept("wl_g%d" % piece, [P, c1 - c0, 4], BF16)
+            grouped = kept("wl_grouped%d" % piece, [P, c1 - c0, PACK], BF16)
             nc.scalar.copy(out=grouped[:], in_=raw.rearrange("p j c -> p c j"))
             quantize(wl_c[:, c0:c1], wl_s[:, c0:c1], grouped[:].rearrange("p c j -> p (c j)"))
 
@@ -84,74 +87,86 @@ def tile_list_binocular_fusion_readout_kernel(
         nc.sync.dma_start(idx_a[:], offs2)
         nc.sync.dma_start(idx_b[:], offs3)
         load_scale_rows(nc.sync, tab_s, tab_scales)
-        wl_first = kept("wl_first", [P, 4, WL_FIRST], F32)
+        wl_first = kept("wide", [P, PACK, WL_FIRST], F32)
         load_k_first(wl_first[:], wl[:, :WL_FIRST])
-        tab_w = kept("tab_w", [P, T], I32)
+        tab_w = kept("table_words", [P, T], I32)
         nc.sync.dma_start(out=tab_w[:], in_=tab_words[0].rearrange("p t i -> p (t i)").bitcast(I32))
         quantize_wl(0, wl_first[:])
-        gains = kept("wl_g0", [P, 2 * S + 2 * T2], F32)
-        gain_a, gain_b, stream = gains[:, :S], gains[:, S : 2 * S], gains[:, 2 * S :]
+        inputs = kept("wide", [P, 2 * S + 2 * T2], F32)
+        gain_a, gain_b, stream = inputs[:, :S], inputs[:, S : 2 * S], inputs[:, 2 * S :]
         nc.sync.dma_start(out=gain_a, in_=wg1)
         nc.sync.dma_start(out=gain_b, in_=wg2)
 
-        v_w = kept("v_w", [P, S], U32)
-        v_s = kept("v_s", [P, S], U8)
-        halves = [(slice(BANK * u, BANK * (u + 1)), slice(32 * u, 32 * (u + 1))) for u in range(2)]
-        for entries, columns in halves:
-            nc.vector.tensor_copy(v_s[:, entries], tab_s[:].indirect(idx[:, columns]))
-        for entries, columns in halves:
-            nc.vector.tensor_copy(v_w[:, entries], tab_w[:].bitcast(U32).indirect(idx[:, columns]))
+        v_w = kept("picked_words", [P, S], U32)
+        v_s = kept("picked_scales", [P, S], U8)
+        halves = ((0, BANK), (BANK, S))
+        head_and_rest = ((0, HEAD), (HEAD, S))
+        for e0, e1 in halves:
+            nc.vector.tensor_copy(v_s[:, e0:e1], tab_s[:].indirect(entries(idx, e0, e1)))
+        for e0, e1 in head_and_rest:
+            nc.vector.tensor_copy(v_w[:, e0:e1], tab_w[:].bitcast(U32).indirect(entries(idx, e0, e1)))
 
-        wr_s = kept("tab_s", [P, H], U8)
+        wr_s = kept("table_scales", [P, H], U8)
         nc.gpsimd.memset(wr_s[:].bitcast(I32), 0)
         load_scale_rows(nc.gpsimd, wr_s, wr_scales)
-        page_b = kept("tab_w", [P, T2], F32)
+        page_b = kept("table_words", [P, T2], F32)
         nc.gpsimd.memset(page_b[:], 0.0)
-        wr_w = kept("wr_w", [P, 2 * H], U8)
+        wr_w = kept("wl_grouped0", [P, 2 * H], U8)
         nc.sync.dma_start(out=wr_w[:].bitcast(I32), in_=wr_words[0].bitcast(I32))
-        wd_g = kept("wd_g", [P, 2, 4 * N], BF16)
+        wd_g = kept("wd_grouped", [P, 2, PACK * N], BF16)
         rest_rows = {}
 
-        def load_rest(s, slot):
-            rest_rows[s] = stream[:, T2 * slot : T2 * (slot + 1)]
+        def load_rest(s):
+            place = s % 2
+            rest_rows[s] = stream[:, T2 * place : T2 * (place + 1)]
             nc.sync.dma_start(out=rest_rows[s], in_=rest[P * s : P * (s + 1), :])
 
-        def load_wl(piece, slot):
+        def load_wl(piece):
             c0, c1 = WL_PIECES[piece]
-            raw = stream[:, T2 * slot : T2 * slot + 4 * (c1 - c0)].rearrange("p (j c) -> p j c", j=4)
+            raw = stream[:, T2 : T2 + PACK * (c1 - c0)].rearrange("p (j c) -> p j c", j=PACK)
             load_k_first(raw, wl[:, c0:c1])
             quantize_wl(piece, raw)
 
-        def load_wd(b, slot):
-            raw = stream[:, T2 * slot : T2 * slot + 4 * N].rearrange("p (j c) -> p j c", j=4)
+        def load_wd(b):
+            raw = stream[:, : PACK * N].rearrange("p (j c) -> p j c", j=PACK)
             load_k_first(raw, wd[K * b : K * (b + 1), :])
-            nc.scalar.copy(out=wd_g[:, b, :].rearrange("p (c j) -> p c j", j=4), in_=raw.rearrange("p j c -> p c j"))
+            nc.scalar.copy(
+                out=wd_g[:, b, :].rearrange("p (c j) -> p c j", j=PACK), in_=raw.rearrange("p j c -> p c j")
+            )
 
-        load_rest(0, 0)
-        load_wl(1, 1)
-        load_rest(1, 1)
+        load_rest(0)
+        load_wl(1)
+        load_rest(1)
 
-        def drive(targets, codes, scales):
-            for bank, target, (entries, columns) in zip(h_banks, targets, halves):
+        def drive(parts, codes, scales):
+            for bank, target, e0, e1 in parts:
                 nc.tensor.matmul_mx(
-                    out=bank[:], lhsT=codes, lhsT_scale=scales,
-                    rhs=v_w[:, entries].bitcast(FP8X4), rhs_scale=v_s[:, entries], start=True, stop=True,
+                    out=bank[:, : e1 - e0], lhsT=codes, lhsT_scale=scales,
+                    rhs=v_w[:, e0:e1].bitcast(FP8X4), rhs_scale=v_s[:, e0:e1], start=True, stop=True,
                 )
-                nc.scalar.copy(out=target, in_=bank[:])
+                nc.scalar.copy(out=target, in_=bank[:, : e1 - e0])
 
         def drive_a(s):
             h = ring.tile([P, S], F32, name="h_a", tag="h_a")
-            drive([h[:, :BANK], h[:, BANK:]], wl_c[:, P * s : P * (s + 1)].bitcast(FP8X4), wl_s[:, P * s : P * (s + 1)])
+            cuts = [(h_banks[0], 0, BANK), (h_banks[1], BANK, S)]
+            if s == 0:
+                cuts = [(turn_banks[0], 0, HEAD), (h_banks[0], HEAD, BANK), cuts[1]]
+            parts = [(bank, h[:, e0:e1], e0, e1) for bank, e0, e1 in cuts]
+            drive(parts, wl_c[:, P * s : P * (s + 1)].bitcast(FP8X4), wl_s[:, P * s : P * (s + 1)])
             return h
 
         def drive_b(s):
             if s + 1 < SLICES:
                 h = ring.tile([P, S], F32, name="h_b", tag="h_b")
-                targets = [h[:, :BANK], h[:, BANK:]]
+                targets = [h[:, e0:e1] for e0, e1 in halves]
             else:
                 h = targets = [kept("h_last%d" % u, [P, BANK], F32)[:] for u in range(2)]
-            drive(targets, wr_w[:, 2 * P * s : 2 * P * (s + 1)].bitcast(FP4X4), wr_s[:, P * s : P * (s + 1)])
+            parts = [(bank, target, e0, e1) for bank, target, (e0, e1) in zip(h_banks, targets, halves)]
+            drive(parts, wr_w[:, 2 * P * s : 2 * P * (s + 1)].bitcast(FP4X4), wr_s[:, P * s : P * (s + 1)])
             return h
+
+        def scatter(page, offsets, h, gain):
+            nc.vector.tensor_tensor(page[:].indirect(offsets), h, gain, mybir.AluOpType.mult)
 
         def add_turned(source, c, first=False, last=False):
             for j in range(TILES):
@@ -170,32 +185,26 @@ def tile_list_binocular_fusion_readout_kernel(
             nc.scalar.activation(
                 out=z_turned[b, c][:, :, :, 32 * q : 32 * (q + 1), :].rearrange("m j u p e -> m u j p e"),
                 in_=sum_banks[c][:].rearrange("m (j p u e) -> m u j p e", j=TILES, u=2, e=2),
-                func=SQUARE,
+                func=mybir.ActivationFunctionType.Square,
             )
 
         def turn_back(b, c, pair, grouped, copies):
             words = z_turned[b, c][:].rearrange("m j u p e -> m (j u p e)").bitcast(F32)
             target = grouped[:].bitcast(F32).rearrange("p (h j m u) -> p h j m u", h=2, j=2, u=2)
             for half in range(2):
-                for i in range(4):
+                for i in range(TILES):
                     w0 = BANK * half + P * i
                     nc.tensor.transpose(pair[half][:, P * i : P * (i + 1)], words[:, w0 : w0 + P], ident[:])
-                copies[half](
-                    out=target[:, half], in_=pair[half][:].rearrange("p (j u m) -> p j m u", j=2, u=2)
-                )
+                copies[half](out=target[:, half], in_=pair[half][:].rearrange("p (j u m) -> p j m u", j=2, u=2))
 
-        def scatter(page, offsets, h, gain):
-            nc.vector.tensor_tensor(page[:].indirect(offsets), h, gain, MULT)
-
-        z_g = {}
-        wd_s = kept("wd_s", [P, 2, N], U8)
-        z_s = kept("z_s", [P, 2, T2], U8)
-        wd_c, z_c = {}, {}
+        z_g, z_c, wd_c = {}, {}, {}
+        wd_s = kept("wd_scales", [P, 2, N], U8)
+        z_s = kept("z_scales", [P, 2, T2], U8)
         out_banks = ((banks[4], banks[5], banks[6]), (banks[3], banks[7], banks[0]))
 
         def quantize_wd(b):
             for n0, n1 in ((0, 2 * P), (2 * P, N)):
-                quantize(wd_c[b][:, n0:n1], wd_s[:, b, n0:n1], wd_g[:, b, 4 * n0 : 4 * n1])
+                quantize(wd_c[b][:, n0:n1], wd_s[:, b, n0:n1], wd_g[:, b, PACK * n0 : PACK * n1])
 
         def quantize_z(b, c):
             quantize(z_c[b, c], z_s[:, b, BANK * c : BANK * (c + 1)], z_g[b, c][:])
@@ -212,8 +221,8 @@ def tile_list_binocular_fusion_readout_kernel(
         h_a, h_b = drive_a(0), drive_b(0)
         for s in range(SLICES):
             if s == 0:
-                for entries, columns in halves:
-                    scatter(page_a, idx_a[:, columns], h_a[:, entries], gain_a[:, entries])
+                for e0, e1 in head_and_rest:
+                    scatter(page_a, entries(idx_a, e0, e1), h_a[:, e0:e1], gain_a[:, e0:e1])
             else:
                 scatter(page_a, idx_a[:], h_a[:], gain_a)
                 for c in range(CHUNKS):
@@ -224,12 +233,12 @@ def tile_list_binocular_fusion_readout_kernel(
             for c in range(CHUNKS):
                 add_turned(rest_rows[s], c, first=True)
             if s == 1:
-                load_wl(2, 1)
+                load_wl(2)
             if s + 2 < SLICES:
-                load_rest(s + 2, s % 2)
+                load_rest(s + 2)
             if s == SLICES - 2:
-                load_wd(0, 0)
-                load_wd(1, 0)
+                load_wd(0)
+                load_wd(1)
             if s + 1 < SLICES:
                 scatter(page_b, idx_b[:], h_b[:], gain_b)
             for c in range(CHUNKS):
@@ -238,25 +247,30 @@ def tile_list_binocular_fusion_readout_kernel(
                 h_b = drive_b(s + 1)
             if s in (PASS_SLICES, PASS_SLICES + 1):
                 for c in (2 * (s - PASS_SLICES), 2 * (s - PASS_SLICES) + 1):
-                    z_g[0, c] = kept("z_g0_%d" % c, [P, 4 * BANK], BF16)
+                    z_g[0, c] = kept("z_grouped0_%d" % c, [P, PACK * BANK], BF16)
                     turn_back(0, c, turn_banks, z_g[0, c], (nc.scalar.copy, nc.scalar.copy))
 
-        (entries, columns), (last_entries, last_columns) = halves
-        scatter(page_b, idx_b[:, columns], h_b[0], gain_b[:, entries])
+        scatter(page_b, entries(idx_b, 0, BANK), h_b[0], gain_b[:, :BANK])
         early_c = kept("h_last0", [P, N + BANK], U32)
         wd_c[0], z_c[0, 0] = early_c[:, :N], early_c[:, N:]
         quantize_wd(0)
         quantize_z(0, 0)
         read_out(0, 0)
-        scatter(page_b, idx_b[:, last_columns], h_b[1], gain_b[:, last_entries])
+        scatter(page_b, entries(idx_b, BANK, S), h_b[1], gain_b[:, BANK:])
 
-        late_c = kept("wl_g0", [P, N + T2 - BANK], U32)
+        late_c = kept("wide", [P, N + T2 - BANK], U32)
         wd_c[1] = late_c[:, :N]
-        z1_c = kept("z1_c", [P, T2], U32)
+        z1_c = kept("z_codes1", [P, T2], U32)
         for c in range(CHUNKS):
             z_c[1, c] = z1_c[:, BANK * c : BANK * (c + 1)]
             if c > 0:
                 z_c[0, c] = late_c[:, N + BANK * (c - 1) : N + BANK * c]
+
+        def turn_last(c):
+            z_g[1, c] = ring.tile([P, PACK * BANK], BF16, name="z_grouped1", tag="z_grouped1", align_bytes=64)
+            pair = (banks[7], banks[0]) if c == 0 else banks[1:3]
+            turn_back(1, c, pair, z_g[1, c], (nc.scalar.copy, nc.vector.tensor_copy))
+            quantize_z(1, c)
 
         def store(c):
             for t, bank in enumerate(out_banks[c % 2]):
@@ -265,12 +279,6 @@ def tile_list_binocular_fusion_readout_kernel(
                 copy(out=staged[:], in_=bank[:])
                 nc.sync.dma_start(out=out[P * t : P * (t + 1), BANK * c : BANK * (c + 1)], in_=staged[:])
 
-        def turn_last(c):
-            z_g[1, c] = ring.tile([P, 4 * BANK], BF16, name="z_g1", tag="z_g1", align_bytes=64)
-            pair = (banks[7], banks[0]) if c == 0 else banks[1:3]
-            turn_back(1, c, pair, z_g[1, c], (nc.scalar.copy, nc.vector.tensor_copy))
-            quantize_z(1, c)
-
         quantize_z(0, 1)
         quantize_wd(1)
         quantize_z(0, 2)
@@ -278,18 +286,14 @@ def tile_list_binocular_fusion_readout_kernel(
             add_turned(page_b, c, last=True)
             square(SLICES - 1, c)
         turn_last(0)
-        turn_last(1)
-        read_out(0, 1)
-        read_out(1, 0)
-        store(0)
-        turn_last(2)
-        quantize_z(0, 3)
-        read_out(1, 1)
-        store(1)
-        read_out(0, 2)
-        turn_last(3)
-        read_out(1, 2)
-        store(2)
-        read_out(0, 3)
-        read_out(1, 3)
-        store(3)
+        for c in range(CHUNKS):
+            if c + 1 < CHUNKS:
+                turn_last(c + 1)
+            if c == 0:
+                read_out(0, 1)
+            if c == 1:
+                quantize_z(0, CHUNKS - 1)
+            read_out(1, c)
+            store(c)
+            if 0 < c < CHUNKS - 1:
+                read_out(0, c + 1)

from contextlib import ExitStack

import concourse.mybir as mybir

K, T, S, T2, H, N = 512, 2048, 1024, 2048, 1024, 384
FLOPS = 2 * 2 * K * H * S + 2 * H * N * T2

F32 = mybir.dt.float32
BF16 = mybir.dt.bfloat16
I32 = mybir.dt.int32
U32 = mybir.dt.uint32
U16 = mybir.dt.uint16
U8 = mybir.dt.uint8
FP8X4 = mybir.dt.float8_e4m3fn_x4
FP4X4 = mybir.dt.float4_e2m1fn_x4

P = 128
PACK = 4
BANK = 512
PER_COLUMN = 16
SLICES = H // P
PASS_SLICES = 4
CHUNKS = T2 // BANK
TILES = BANK // P
WL_PIECES = ((0, 256), (256, 512), (512, 1024))
WL_FIRST = WL_PIECES[0][1]
HEAD = 256


def tile_list_binocular_fusion_readout_kernel(
    tc, tab_words, tab_scales, offs, wl, wr_words, wr_scales, offs2, offs3, wg1, wg2, rest, wd, out
):
    nc = tc.nc
    with ExitStack() as ctx:
        lists = ctx.enter_context(tc.tile_pool(name="lists", bufs=1))
        keep = ctx.enter_context(tc.tile_pool(name="keep", bufs=1))
        ring = ctx.enter_context(tc.tile_pool(name="ring", bufs=2))
        psum = ctx.enter_context(tc.psum_pool(name="psum", bufs=1))

        def kept(slot, shape, dtype):
            return keep.tile(shape, dtype, name=slot, tag=slot, align_bytes=64)

        banks = [psum.tile([P, BANK], F32, name="bank%d" % b) for b in range(8)]
        sum_banks, h_banks, turn_banks = banks[0:4], banks[4:6], banks[6:8]

        idx = lists.tile([P, S // PER_COLUMN], U16, name="idx")
        idx_a = lists.tile([P, S // PER_COLUMN], U16, name="idx_a")
        idx_b = lists.tile([P, S // PER_COLUMN], U16, name="idx_b")

        def entries(offsets, e0, e1):
            return offsets[:, e0 // PER_COLUMN : e1 // PER_COLUMN]

        def load_scale_rows(queue, plane, rows):
            for q in range(4):
                queue.dma_start(
                    out=plane[32 * q : 32 * q + 4, :].bitcast(I32), in_=rows[0, 4 * q : 4 * q + 4, :].bitcast(I32)
                )

        def load_k_first(raw, rows):
            nc.sync.dma_start(out=raw, in_=rows.rearrange("(p j) c -> p j c", j=PACK))

        def quantize(codes, scales, grouped):
            nc.vector.quantize_mx(out=codes.bitcast(FP8X4), scales=scales, in_=grouped)

        tab_s = kept("table_scales", [P, T], U8)
        ident = kept("ident", [P, P], F32)
        zeros = kept("table_words", [P, P], F32)
        nc.gpsimd.memset(zeros[:], 0.0)
        nc.gpsimd.memset(tab_s[:].bitcast(I32), 0)
        nc.gpsimd.affine_select(
            out=ident[:], in_=zeros[:], pattern=[[-1, P]],
            compare_op=mybir.AluOpType.not_equal, fill=1.0, base=0, channel_multiplier=1,
        )
        page_a = kept("page_a", [P, T2], F32)
        nc.gpsimd.memset(page_a[:], 0.0)

        wl_c = kept("wl_codes", [P, H], U32)
        wl_s = kept("wl_scales", [P, H], U8)

        def quantize_wl(piece, raw):
            c0, c1 = WL_PIECES[piece]
            grouped = kept("wl_grouped%d" % piece, [P, c1 - c0, PACK], BF16)
            nc.scalar.copy(out=grouped[:], in_=raw.rearrange("p j c -> p c j"))
            quantize(wl_c[:, c0:c1], wl_s[:, c0:c1], grouped[:].rearrange("p c j -> p (c j)"))

        nc.sync.dma_start(idx[:], offs)
        nc.sync.dma_start(idx_a[:], offs2)
        nc.sync.dma_start(idx_b[:], offs3)
        load_scale_rows(nc.sync, tab_s, tab_scales)
        wl_first = kept("wide", [P, PACK, WL_FIRST], F32)
        load_k_first(wl_first[:], wl[:, :WL_FIRST])
        tab_w = kept("table_words", [P, T], I32)
        nc.sync.dma_start(out=tab_w[:], in_=tab_words[0].rearrange("p t i -> p (t i)").bitcast(I32))
        quantize_wl(0, wl_first[:])
        inputs = kept("wide", [P, 2 * S + 2 * T2], F32)
        gain_a, gain_b, stream = inputs[:, :S], inputs[:, S : 2 * S], inputs[:, 2 * S :]
        nc.sync.dma_start(out=gain_a, in_=wg1)
        nc.sync.dma_start(out=gain_b, in_=wg2)

        v_w = kept("picked_words", [P, S], U32)
        v_s = kept("picked_scales", [P, S], U8)
        halves = ((0, BANK), (BANK, S))
        head_and_rest = ((0, HEAD), (HEAD, S))
        for e0, e1 in halves:
            nc.vector.tensor_copy(v_s[:, e0:e1], tab_s[:].indirect(entries(idx, e0, e1)))
        for e0, e1 in head_and_rest:
            nc.vector.tensor_copy(v_w[:, e0:e1], tab_w[:].bitcast(U32).indirect(entries(idx, e0, e1)))

        wr_s = kept("table_scales", [P, H], U8)
        nc.gpsimd.memset(wr_s[:].bitcast(I32), 0)
        load_scale_rows(nc.gpsimd, wr_s, wr_scales)
        page_b = kept("table_words", [P, T2], F32)
        nc.gpsimd.memset(page_b[:], 0.0)
        wr_w = kept("wl_grouped0", [P, 2 * H], U8)
        nc.sync.dma_start(out=wr_w[:].bitcast(I32), in_=wr_words[0].bitcast(I32))
        wd_g = kept("wd_grouped", [P, 2, PACK * N], BF16)
        rest_rows = {}

        def load_rest(s):
            place = s % 2
            rest_rows[s] = stream[:, T2 * place : T2 * (place + 1)]
            nc.sync.dma_start(out=rest_rows[s], in_=rest[P * s : P * (s + 1), :])

        def load_wl(piece):
            c0, c1 = WL_PIECES[piece]
            raw = stream[:, T2 : T2 + PACK * (c1 - c0)].rearrange("p (j c) -> p j c", j=PACK)
            load_k_first(raw, wl[:, c0:c1])
            quantize_wl(piece, raw)

        def load_wd(b):
            raw = stream[:, : PACK * N].rearrange("p (j c) -> p j c", j=PACK)
            load_k_first(raw, wd[K * b : K * (b + 1), :])
            nc.scalar.copy(
                out=wd_g[:, b, :].rearrange("p (c j) -> p c j", j=PACK), in_=raw.rearrange("p j c -> p c j")
            )

        load_rest(0)
        load_wl(1)
        load_rest(1)

        def drive(parts, codes, scales):
            for bank, target, e0, e1 in parts:
                nc.tensor.matmul_mx(
                    out=bank[:, : e1 - e0], lhsT=codes, lhsT_scale=scales,
                    rhs=v_w[:, e0:e1].bitcast(FP8X4), rhs_scale=v_s[:, e0:e1], start=True, stop=True,
                )
                nc.scalar.copy(out=target, in_=bank[:, : e1 - e0])

        def drive_a(s):
            h = ring.tile([P, S], F32, name="h_a", tag="h_a")
            cuts = [(h_banks[0], 0, BANK), (h_banks[1], BANK, S)]
            if s == 0:
                cuts = [(turn_banks[0], 0, HEAD), (h_banks[0], HEAD, BANK), cuts[1]]
            parts = [(bank, h[:, e0:e1], e0, e1) for bank, e0, e1 in cuts]
            drive(parts, wl_c[:, P * s : P * (s + 1)].bitcast(FP8X4), wl_s[:, P * s : P * (s + 1)])
            return h

        def drive_b(s):
            if s + 1 < SLICES:
                h = ring.tile([P, S], F32, name="h_b", tag="h_b")
                targets = [h[:, e0:e1] for e0, e1 in halves]
            else:
                h = targets = [kept("h_last%d" % u, [P, BANK], F32)[:] for u in range(2)]
            parts = [(bank, target, e0, e1) for bank, target, (e0, e1) in zip(h_banks, targets, halves)]
            drive(parts, wr_w[:, 2 * P * s : 2 * P * (s + 1)].bitcast(FP4X4), wr_s[:, P * s : P * (s + 1)])
            return h

        def scatter(page, offsets, h, gain):
            nc.vector.tensor_tensor(page[:].indirect(offsets), h, gain, mybir.AluOpType.mult)

        def add_turned(source, c, first=False, last=False):
            for j in range(TILES):
                m0 = BANK * c + P * j
                nc.tensor.matmul(
                    sum_banks[c][:, P * j : P * (j + 1)], source[:, m0 : m0 + P], ident[:],
                    start=(first and j == 0), stop=(last and j == TILES - 1), is_transpose=True,
                )

        z_turned = {}

        def square(s, c):
            b, q = divmod(s, PASS_SLICES)
            if q == 0:
                z_turned[b, c] = kept("z_turned%d_%d" % (b, c), [P, TILES, 2, P, 2], BF16)
            nc.scalar.activation(
                out=z_turned[b, c][:, :, :, 32 * q : 32 * (q + 1), :].rearrange("m j u p e -> m u j p e"),
                in_=sum_banks[c][:].rearrange("m (j p u e) -> m u j p e", j=TILES, u=2, e=2),
                func=mybir.ActivationFunctionType.Square,
            )

        def turn_back(b, c, pair, grouped, copies):
            words = z_turned[b, c][:].rearrange("m j u p e -> m (j u p e)").bitcast(F32)
            target = grouped[:].bitcast(F32).rearrange("p (h j m u) -> p h j m u", h=2, j=2, u=2)
            for half in range(2):
                for i in range(TILES):
                    w0 = BANK * half + P * i
                    nc.tensor.transpose(pair[half][:, P * i : P * (i + 1)], words[:, w0 : w0 + P], ident[:])
                copies[half](out=target[:, half], in_=pair[half][:].rearrange("p (j u m) -> p j m u", j=2, u=2))

        z_g, z_c, wd_c = {}, {}, {}
        wd_s = kept("wd_scales", [P, 2, N], U8)
        z_s = kept("z_scales", [P, 2, T2], U8)
        out_banks = ((banks[4], banks[5], banks[6]), (banks[3], banks[7], banks[0]))

        def quantize_wd(b):
            for n0, n1 in ((0, 2 * P), (2 * P, N)):
                quantize(wd_c[b][:, n0:n1], wd_s[:, b, n0:n1], wd_g[:, b, PACK * n0 : PACK * n1])

        def quantize_z(b, c):
            quantize(z_c[b, c], z_s[:, b, BANK * c : BANK * (c + 1)], z_g[b, c][:])

        def read_out(b, c):
            for t, bank in enumerate(out_banks[c % 2]):
                n = slice(P * t, P * (t + 1))
                nc.tensor.matmul_mx(
                    out=bank[:], lhsT=wd_c[b][:, n].bitcast(FP8X4), lhsT_scale=wd_s[:, b, n],
                    rhs=z_c[b, c].bitcast(FP8X4), rhs_scale=z_s[:, b, BANK * c : BANK * (c + 1)],
                    start=(b == 0), stop=(b == 1),
                )

        h_a, h_b = drive_a(0), drive_b(0)
        for s in range(SLICES):
            if s == 0:
                for e0, e1 in head_and_rest:
                    scatter(page_a, entries(idx_a, e0, e1), h_a[:, e0:e1], gain_a[:, e0:e1])
            else:
                scatter(page_a, idx_a[:], h_a[:], gain_a)
                for c in range(CHUNKS):
                    add_turned(page_b, c, last=True)
                    square(s - 1, c)
            if s + 1 < SLICES:
                h_a = drive_a(s + 1)
            for c in range(CHUNKS):
                add_turned(rest_rows[s], c, first=True)
            if s == 1:
                load_wl(2)
            if s + 2 < SLICES:
                load_rest(s + 2)
            if s == SLICES - 2:
                load_wd(0)
                load_wd(1)
            if s + 1 < SLICES:
                scatter(page_b, idx_b[:], h_b[:], gain_b)
            for c in range(CHUNKS):
                add_turned(page_a, c)
            if s + 1 < SLICES:
                h_b = drive_b(s + 1)
            if s in (PASS_SLICES, PASS_SLICES + 1):
                for c in (2 * (s - PASS_SLICES), 2 * (s - PASS_SLICES) + 1):
                    z_g[0, c] = kept("z_grouped0_%d" % c, [P, PACK * BANK], BF16)
                    turn_back(0, c, turn_banks, z_g[0, c], (nc.scalar.copy, nc.scalar.copy))

        scatter(page_b, entries(idx_b, 0, BANK), h_b[0], gain_b[:, :BANK])
        early_c = kept("h_last0", [P, N + BANK], U32)
        wd_c[0], z_c[0, 0] = early_c[:, :N], early_c[:, N:]
        quantize_wd(0)
        quantize_z(0, 0)
        read_out(0, 0)
        scatter(page_b, entries(idx_b, BANK, S), h_b[1], gain_b[:, BANK:])

        late_c = kept("wide", [P, N + T2 - BANK], U32)
        wd_c[1] = late_c[:, :N]
        z1_c = kept("z_codes1", [P, T2], U32)
        for c in range(CHUNKS):
            z_c[1, c] = z1_c[:, BANK * c : BANK * (c + 1)]
            if c > 0:
                z_c[0, c] = late_c[:, N + BANK * (c - 1) : N + BANK * c]

        def turn_last(c):
            z_g[1, c] = ring.tile([P, PACK * BANK], BF16, name="z_grouped1", tag="z_grouped1", align_bytes=64)
            pair = (banks[7], banks[0]) if c == 0 else banks[1:3]
            turn_back(1, c, pair, z_g[1, c], (nc.scalar.copy, nc.vector.tensor_copy))
            quantize_z(1, c)

        def store(c):
            for t, bank in enumerate(out_banks[c % 2]):
                staged = ring.tile([P, BANK], F32, name="staged", tag="staged", bufs=6)
                copy = nc.vector.tensor_copy if t == 1 else nc.scalar.copy
                copy(out=staged[:], in_=bank[:])
                nc.sync.dma_start(out=out[P * t : P * (t + 1), BANK * c : BANK * (c + 1)], in_=staged[:])

        quantize_z(0, 1)
        quantize_wd(1)
        quantize_z(0, 2)
        for c in range(CHUNKS):
            add_turned(page_b, c, last=True)
            square(SLICES - 1, c)
        turn_last(0)
        for c in range(CHUNKS):
            if c + 1 < CHUNKS:
                turn_last(c + 1)
            if c == 0:
                read_out(0, 1)
            if c == 1:
                quantize_z(0, CHUNKS - 1)
            read_out(1, c)
            store(c)
            if 0 < c < CHUNKS - 1:
                read_out(0, c + 1)
